import numpy as np
import ml_dtypes


def mxq(x, axis, fmt="e4m3"):
    dtype, down = {"e4m3": (ml_dtypes.float8_e4m3fn, 7), "e5m2": (ml_dtypes.float8_e5m2, 14)}[fmt]
    v = np.moveaxis(np.asarray(x, np.float32).astype(ml_dtypes.bfloat16).astype(np.float64), axis, -1)
    blocks = v.reshape(v.shape[:-1] + (-1, 32))
    amax = np.abs(blocks).max(-1, keepdims=True)
    byte = np.maximum(np.where(amax > 0, np.frexp(amax)[1] - 1 + 127, 0) - down, 1)
    scale = np.exp2(byte - 127.0)
    codes = (blocks / scale).astype(np.float32).astype(dtype).astype(np.float64)
    return np.moveaxis((codes * scale).reshape(v.shape), -1, axis)


WIDE = False


def mx_kscale(k):
    if not WIDE:
        return np.ones(k)
    levels = np.array([10, -10, 5, -5, 0])
    if k % 512:
        return np.exp2(np.random.permutation(np.resize(levels, k // 32))).repeat(32)
    a = np.empty((k // 512, 16))
    for p in range(k // 512):
        a[p, :8] = np.random.permutation(np.resize(levels, 8))
        for g in range(8):
            far = levels[np.abs(levels - a[p, g]) >= 10]
            a[p, g + 8] = far[np.random.randint(len(far))]
    return np.exp2(a.ravel()).repeat(32)


BF16 = ml_dtypes.bfloat16


def bf(x):
    return np.asarray(x, np.float32).astype(BF16)


def f64(x):
    return np.asarray(x).astype(np.float64)


E2M1 = np.array([0.0, 0.5, 1.0, 1.5, 2.0, 3.0, 4.0, 6.0, -0.0, -0.5, -1.0, -1.5, -2.0, -3.0, -4.0, -6.0])


def pack_weight(w, fmt):
    k, n = w.shape
    w = f64(bf(w)).reshape(k // 32, 32, n)
    amax = np.abs(w).max(1)
    if fmt == "e4m3":
        byte = np.frexp(amax)[1] - 1 + 127 - 7
    else:
        mant, ex = np.frexp(amax / 6.0)
        byte = np.where(mant > 0.5, ex, ex - 1) + 127
    byte = np.clip(np.where(amax > 0, byte, 1), 1, 254)
    scaled = (w * np.exp2(127.0 - byte)[:, None, :]).reshape(k, n).astype(np.float32)
    by_word = np.ascontiguousarray(scaled.reshape(k // 512, 128, 4, n).transpose(0, 1, 3, 2))
    if fmt == "e4m3":
        words = by_word.astype(ml_dtypes.float8_e4m3fn).view(np.uint8)
    else:
        c = by_word.astype(ml_dtypes.float4_e2m1fn).view(np.uint8) & 0xF
        words = c[..., 0::2] | (c[..., 1::2] << 4)
    return np.ascontiguousarray(words), np.ascontiguousarray(byte.astype(np.uint8).reshape(k // 512, 16, n))


def unpack_weight(words, scales, fmt):
    g, p, n, _ = words.shape
    if fmt == "e4m3":
        vals = np.ascontiguousarray(words).view(ml_dtypes.float8_e4m3fn).astype(np.float64)
    else:
        nib = np.empty((g, p, n, 4), np.uint8)
        nib[..., 0::2] = words & 0xF
        nib[..., 1::2] = words >> 4
        vals = E2M1[nib]
    vals = vals * np.repeat(np.exp2(scales.astype(np.float64) - 127.0), 8, axis=1)[..., None]
    return vals.transpose(0, 1, 3, 2).reshape(g * 512, n)

E4M3FN = np.array([(-1.0 if i & 128 else 1.0) * ((1.0 + (i & 7) / 8.0) * 2.0 ** (((i >> 3) & 15) - 7) if i & 120 else (i & 7) * 2.0 ** -9) for i in range(256)])


def e4m3fn_bytes(y):
    return np.clip(np.asarray(y, np.float64), -448.0, 448.0).astype(np.float32).astype(ml_dtypes.float8_e4m3fn).view(np.uint8)


def e4m3fn_values(b):
    return E4M3FN[b]


T, D = 1024, 1024


def draw0():
    s = mx_kscale(D)
    t = mx_kscale(D)
    inv = 1.0 / np.sqrt(D)
    r = np.where(np.random.random((T, 1)) < 0.25, 0.001, 1.0)
    x = bf((0.5 + 1.5 * np.random.standard_normal((T, D))) * r)
    c = bf(np.random.standard_normal((T, D)) * s)
    wsc_words, wsc_scales = pack_weight(np.random.standard_normal((D, D)) * 0.5 * inv / s[:, None] * t, "e4m3")
    bsc = bf((1.0 + 0.1 * np.random.standard_normal(D)) * t)
    wsh_words, wsh_scales = pack_weight(np.random.standard_normal((D, D)) * 0.5 * inv / s[:, None] * t, "e4m3")
    wg_words, wg_scales = pack_weight(np.random.standard_normal((D, D)) * inv / s[:, None], "e4m3")
    w_words, w_scales = pack_weight(np.random.standard_normal((D, D)) * inv / t[:, None], "e4m3")
    return {
        "x": x,
        "c": c,
        "wsc_words": wsc_words,
        "wsc_scales": wsc_scales,
        "bsc": bsc,
        "wsh_words": wsh_words,
        "wsh_scales": wsh_scales,
        "wg_words": wg_words,
        "wg_scales": wg_scales,
        "w_words": w_words,
        "w_scales": w_scales,
    }


def _normalize(x):
    mean = np.mean(x, axis=-1, keepdims=True)
    centered = x - mean
    var = np.mean(centered * centered, axis=-1, keepdims=True)
    return centered / np.sqrt(var + 1e-6)


def core(x, c, wsc_words, wsc_scales, bsc, wsh_words, wsh_scales, wg_words, wg_scales, w_words, w_scales):
    x = f64(x)
    n = _normalize(x)
    cq = mxq(f64(c), 1, "e4m3")
    scale = (cq @ unpack_weight(wsc_words, wsc_scales, "e4m3")) + f64(bsc)
    shift = cq @ unpack_weight(wsh_words, wsh_scales, "e4m3")
    gate = cq @ unpack_weight(wg_words, wg_scales, "e4m3")
    y = n * scale + shift
    f = mxq(y, 1, "e4m3") @ unpack_weight(w_words, w_scales, "e4m3")
    return x + gate * f


def setup_inputs():
    drawn = draw0()
    full = np.asarray(drawn['c']).astype(np.float64)
    scale = (np.abs(full).reshape(8, 128, 8, 128).max(axis=(1, 3)) / 448.0).astype(np.float32)
    given = {}
    for key, value in drawn.items():
        if key == 'c':
            given['c_bytes'] = e4m3fn_bytes(full / np.repeat(np.repeat(scale.astype(np.float64), 128, axis=0), 128, axis=1))
            given['c_scale'] = scale
        else:
            given[key] = value
    return given


def reference(x, c_bytes, c_scale, wsc_words, wsc_scales, bsc, wsh_words, wsh_scales, wg_words, wg_scales, w_words, w_scales):
    return core(x, e4m3fn_values(c_bytes) * np.repeat(np.repeat(c_scale.astype(np.float64), 128, axis=0), 128, axis=1), wsc_words, wsc_scales, bsc, wsh_words, wsh_scales, wg_words, wg_scales, w_words, w_scales)

from contextlib import ExitStack

import concourse.mybir as mybir
from concourse.masks import make_identity

T, D = 1024, 1024
FLOPS = 4 * 2 * T * D * D
EPS = 1e-6

F32 = mybir.dt.float32
BF16 = mybir.dt.bfloat16
U32 = mybir.dt.uint32
I32 = mybir.dt.int32
U8 = mybir.dt.uint8
FP8 = mybir.dt.float8_e4m3fn
FP8X4 = mybir.dt.float8_e4m3fn_x4
ALU = mybir.AluOpType
ACT = mybir.ActivationFunctionType

P = 128
TILES = T // P
HALF = 512
BANKS = 8

LOADS = [('cs', 0, 0), ('c', 0, 1), ('plane', 'sc', 0), ('plane', 'sc', 1), ('plane', 'sc', 2), ('plane', 'sc', 3), ('w', 'sc', 0), ('bias', 0, 0), ('c', 1, 3), ('c', 3, 5), ('x', 0, 1), ('w', 'sc', 1), ('plane', 'f', 0), ('plane', 'sh', 0), ('w', 'sh', 0), ('x', 1, 2), ('plane', 'sh', 1), ('plane', 'g', 0), ('plane', 'sh', 2), ('c', 5, 8), ('plane', 'g', 1), ('plane', 'sh', 3), ('w', 'sh', 1), ('plane', 'g', 2), ('plane', 'g', 3), ('plane', 'f', 1), ('x', 2, 3), ('w', 'g', 0), ('w', 'g', 1), ('w', 'f', 0), ('x', 3, 4), ('plane', 'f', 2), ('plane', 'f', 3), ('x', 6, 8), ('w', 'f', 1), ('x', 4, 6)]
POOL_PLANES = ()
WIDEN_ON_VECTOR = (0, 1, 3)
BN_ON_VECTOR = (0, 1, 2)
SUM_ON_VECTOR = ()
ADD_ON_VECTOR = (10, 13, 14, 15)
WARM = 4
Q34 = (4,)
BIAS_ON_POOL = (1, 2, 3, 13)
WARM_TILES = (0, 0)
ORDER = [
    ('Wd', (1,), 0), ('Wd', (0,), 0), ('Tc', (1,), 0), ('Tc', (0,), 0), ('Cc', (1,), 0), ('Cc', (0,), 0),
    ('Mb', (0,), 0), ('Qc', (1,), 0), ('Qc', (0,), 0), ('Wd', (0, 1), 1), ('Wd', (0, 1), 2), ('Msc', (0,), 0),
    ('Wd', (0, 1), 3), ('Tc', (0, 1), 1), ('Cb', (0,), 0), ('St', (0, 1), 0), ('Tc', (0, 1), 2), ('Cc', (0, 1), 1),
    ('Msc', (1,), 0), ('Cc', (0, 1), 2), ('Qc', (0, 1), 1), ('Tc', (0, 1), 3), ('a', (0,), 0), ('rs', (0, 1), 0),
    ('aS', (1,), 0), ('Msc', (1,), 1), ('Qc', (0, 1), 2), ('Wd', (0, 1), 4), ('rc', (0, 1), 0), ('a', (1,), 0),
    ('St', (0, 1), 1), ('Msc', (0,), 1), ('Msc', (1,), 2), ('aS', (1,), 1), ('Msc', (0,), 2), ('b', (0,), 0),
    ('aS', (0,), 1), ('Msh', (0,), 0), ('b', (1,), 0), ('Wd', (0, 1), 6), ('Msh', (0,), 2), ('a', (1,), 2),
    ('a', (0,), 1), ('Msh', (1,), 0), ('c', (0,), 0), ('Wd', (0, 1), 7), ('Msh', (0,), 1), ('a', (0,), 2),
    ('Tc', (0, 1), 6), ('a', (1,), 1), ('c', (1,), 0), ('rs', (0, 1), 1), ('Tc', (0, 1), 4), ('Cc', (0, 1), 3),
    ('St', (0, 1), 2), ('Ty', (0, 1), 0), ('Cc', (0, 1), 6), ('Mg', (0,), 1), ('Cy', (0, 1), 0), ('Mg', (1,), 0),
    ('rc', (0, 1), 1), ('b', (0,), 1), ('Cc', (0, 1), 4), ('Mg', (0,), 0), ('b', (1,), 1), ('Wd', (0, 1), 5),
    ('Msh', (1,), 1), ('Qy', (0, 1), 0), ('c', (0,), 1), ('Msh', (1,), 2), ('rs', (0, 1), 2), ('Qc', (0, 1), 6),
    ('G', (0,), 0), ('Mf', (0,), 0), ('c', (1,), 1), ('G', (1,), 0), ('Tc', (0, 1), 5), ('rc', (0, 1), 2),
    ('Qc', (0, 1), 4), ('G', (0,), 1), ('b', (1,), 2), ('Ty', (0, 1), 1), ('Mg', (1,), 2), ('Cc', (0, 1), 5),
    ('b', (0,), 2), ('Cy', (0, 1), 1), ('Msc', (1,), 4), ('Qc', (0, 1), 3), ('c', (1,), 2), ('St', (0, 1), 3),
    ('Mf', (1,), 0), ('c', (0,), 2), ('Msc', (0,), 4), ('gf', (1,), 0), ('Msc', (1,), 3), ('Qy', (0, 1), 1),
    ('Msc', (0,), 3), ('gf', (0,), 0), ('Mf', (0,), 1), ('Qc', (0, 1), 5), ('St', (0, 1), 5), ('a', (1,), 3),
    ('add', (0, 1), 0), ('Ty', (0, 1), 2), ('gf', (0,), 1), ('Tc', (0, 1), 7), ('Msh', (0,), 3), ('a', (1,), 4),
    ('a', (0,), 3), ('Msc', (1,), 5), ('a', (0,), 4), ('Cy', (0, 1), 2), ('Mg', (1,), 1), ('b', (1,), 3),
    ('Cc', (0, 1), 7), ('Mf', (1,), 1), ('Qy', (0, 1), 2), ('rs', (0, 1), 3), ('Msh', (1,), 3), ('G', (1,), 1),
    ('Qc', (0, 1), 7), ('b', (0,), 3), ('Mf', (1,), 2), ('St', (0, 1), 4), ('gf', (1,), 1), ('Msc', (1,), 6),
    ('rc', (0, 1), 3), ('Mg', (0,), 2), ('a', (1,), 5), ('add', (0, 1), 1), ('Mg', (1,), 3), ('c', (0,), 3),
    ('Msh', (0,), 4), ('c', (1,), 3), ('G', (1,), 2), ('Msh', (1,), 6), ('G', (0,), 2), ('gf', (1,), 2),
    ('Ty', (0, 1), 3), ('rs', (0, 1), 5), ('aS', (1,), 6), ('Mf', (0,), 2), ('b', (1,), 5), ('rs', (0, 1), 4),
    ('Cy', (0, 1), 3), ('b', (0,), 4), ('Msc', (0,), 5), ('G', (1,), 3), ('b', (1,), 4), ('Msh', (1,), 4),
    ('St', (0, 1), 6), ('Qy', (0, 1), 3), ('Mg', (0,), 3), ('rc', (0, 1), 4), ('a', (1,), 6), ('gf', (0,), 2),
    ('Mg', (1,), 4), ('c', (1,), 4), ('Msc', (0,), 7), ('a', (0,), 5), ('Msh', (0,), 5), ('add', (0, 1), 2),
    ('rc', (0, 1), 5), ('c', (0,), 4), ('Mf', (0,), 3), ('G', (0,), 3), ('a', (0,), 7), ('Mf', (1,), 3),
    ('G', (1,), 4), ('gf', (0,), 3), ('Ty', (0, 1), 4), ('Mg', (0,), 4), ('gf', (1,), 3), ('Cy', (0, 1), 4),
    ('b', (1,), 6), ('Msh', (1,), 5), ('rs', (0, 1), 6), ('G', (0,), 4), ('b', (0,), 5), ('Msc', (0,), 6),
    ('St', (0, 1), 7), ('Qy', (0, 1), 4), ('Mg', (1,), 5), ('c', (1,), 5), ('add', (0, 1), 3), ('Mf', (1,), 4),
    ('c', (0,), 5), ('Mf', (0,), 4), ('a', (0,), 6), ('Ty', (0, 1), 5), ('gf', (1,), 4), ('Mg', (0,), 6),
    ('Cy', (0, 1), 5), ('rc', (0, 1), 6), ('gf', (0,), 4), ('Msh', (0,), 6), ('G', (1,), 5), ('b', (0,), 6),
    ('Msc', (1,), 7), ('rs', (0, 1), 7), ('Qy', (0, 1), 5), ('Mg', (0,), 7), ('c', (1,), 6), ('add', (0,), 4),
    ('Mf', (1,), 5), ('c', (0,), 6), ('G', (0,), 7), ('Mg', (1,), 6), ('a', (1,), 7), ('G', (0,), 6),
    ('Ty', (0, 1), 6), ('gf', (1,), 5), ('G', (1,), 6), ('Msh', (0,), 7), ('rc', (0, 1), 7), ('b', (1,), 7),
    ('Cy', (0, 1), 6), ('Msh', (1,), 7), ('add', (1,), 4), ('b', (0,), 7), ('Mg', (0,), 5), ('Qy', (0, 1), 6),
    ('Mf', (0,), 5), ('c', (0,), 7), ('add', (1,), 5), ('G', (0,), 5), ('Mf', (0,), 6), ('c', (1,), 7),
    ('Ty', (0,), 7), ('gf', (0,), 5), ('Ty', (1,), 7), ('Cy', (0,), 7), ('Mf', (1,), 6), ('gf', (0,), 6),
    ('Cy', (1,), 7), ('Mg', (1,), 7), ('Qy', (0,), 7), ('Qy', (1,), 7), ('add', (0,), 5), ('Mf', (0,), 7),
    ('G', (1,), 7), ('gf', (1,), 6), ('add', (0,), 6), ('Mf', (1,), 7), ('gf', (0,), 7), ('gf', (1,), 7),
    ('add', (1,), 6), ('add', (0,), 7), ('add', (1,), 7),
]


def tile_diffusionforcingpertokenadalnzero_d2p_kernel(
    tc, x, c_bytes, c_scale, wsc_words, wsc_scales, bsc, wsh_words, wsh_scales,
    wg_words, wg_scales, w_words, w_scales, out,
):
    nc = tc.nc
    words = {"sc": wsc_words, "sh": wsh_words, "g": wg_words, "f": w_words}
    scales = {"sc": wsc_scales, "sh": wsh_scales, "g": wg_scales, "f": w_scales}

    with ExitStack() as ctx:
        keep = ctx.enter_context(tc.tile_pool(name="keep", bufs=1))
        psum = ctx.enter_context(tc.psum_pool(name="psum", bufs=1))
        ctx.enter_context(tc.manual_schedule())

        def per_tile(name, width, dtype):
            return [keep.tile([P, width], dtype, name="%s%d" % (name, i), align_bytes=64) for i in range(TILES)]

        free_banks = list(range(BANKS))
        held = {}
        uses = []

        def take_bank(key, width=HALF, dtype=F32):
            b = free_banks.pop(0)
            uses.append(b)
            bank = psum.tile([P, width], dtype, tag="bank%d" % b, name="bank%d_%d" % (b, len(uses)))
            held[key] = (b, bank)
            return bank

        def give_bank(key):
            b, bank = held.pop(key)
            free_banks.append(b)
            return bank

        ident = keep.tile([P, P], F32, name="ident")
        ones = keep.tile([P, P], BF16, name="ones")
        bias_row = keep.tile([P, D], BF16, name="bias_row")
        bias = keep.tile([P, D], BF16, name="bias")
        cs = keep.tile([P, TILES * TILES], F32, name="cs")
        junk_s = keep.tile([P, 2, D], BF16, name="junk_s")
        junk_v = keep.tile([P, D], BF16, name="junk_v")
        planes = {k: keep.tile([P, D], U8, name="plane_" + k, align_bytes=64) for k in words}
        codes = {(k, h): keep.tile([P, 2, HALF], U32, name="w_%s%d" % (k, h), align_bytes=64) for k in words for h in range(2)}
        c_raw = {}
        x_sb = {}
        c_wide = per_tile("c_wide", D, BF16)
        c_turn = per_tile("c_turn", D, BF16)
        c_codes = per_tile("c_codes", D // 4, U32)
        c_plane = per_tile("c_plane", D // 4, U8)
        y_codes = per_tile("y_codes", D // 4, U32)
        y_plane = per_tile("y_plane", D // 4, U8)
        mod = per_tile("mod", D, F32)
        gate = per_tile("gate", D, F32)
        y_rows = per_tile("y_rows", D, BF16)
        y_turn = per_tile("y_turn", D, BF16)
        parts = per_tile("parts", 12, F32)
        mean = per_tile("mean", 2, F32)
        ssq = per_tile("ssq", 1, F32)
        veps = per_tile("veps", 1, F32)
        rstd = per_tile("rstd", 1, F32)

        def load_plane(engine, k, q):
            engine.dma_start(
                out=planes[k][32 * q : 32 * q + 8, :].bitcast(I32),
                in_=scales[k][:, 4 * q : 4 * q + 4, :].bitcast(I32),
            )

        zeros = keep.tile([P, HALF], BF16, name="zeros")
        nc.vector.memset(ones[:], 1.0)
        nc.vector.memset(zeros[:].bitcast(I32), 0)
        nc.vector.memset(planes["sc"][:].bitcast(I32), 0)
        nc.vector.memset(bias_row[:].bitcast(I32), 0)
        for k in ("sh", "g", "f"):
            nc.vector.memset(planes[k][:].bitcast(I32), 0)
        make_identity(nc, ident[:])
        nc.scalar.activation(out=junk_s[:, 0, 0:2], in_=ones[:, 0:2], func=ACT.Sqrt)

        c_view = c_bytes.rearrange("(i p) k -> p i k", p=P)
        x_view = x.rearrange("(i p) k -> p i k", p=P)
        for kind, a, b in LOADS:
            if kind == "cs":
                nc.sync.dma_start(out=cs[:], in_=c_scale.rearrange("a b -> (a b)").partition_broadcast(P))
            elif kind == "bias":
                nc.sync.dma_start(out=bias_row[0:1, :], in_=bsc.rearrange("(o n) -> o n", o=1))
            elif kind == "plane":
                load_plane(nc.sync, a, b)
            elif kind == "c":
                group = keep.tile([P, b - a, D], U8, name="c_raw%d" % a)
                nc.sync.dma_start(out=group[:], in_=c_view[:, a:b, :])
                for i in range(a, b):
                    c_raw[i] = group[:, i - a, :]
            elif kind == "x":
                group = keep.tile([P, b - a, D], BF16, name="x_sb%d" % a)
                nc.sync.dma_start(out=group[:], in_=x_view[:, a:b, :])
                for i in range(a, b):
                    x_sb[i] = group[:, i - a, :]
            else:
                src = words[a].rearrange("g p n t -> p g (n t)")[:, :, 4 * HALF * b : 4 * HALF * (b + 1)]
                nc.sync.dma_start(out=codes[a, b][:].bitcast(I32), in_=src.bitcast(I32))
        for k in POOL_PLANES:
            for q in range(4):
                load_plane(nc.gpsimd, k, q)

        def spread_bias():
            bank = take_bank("bias", D, BF16)
            for h in range(2):
                nc.tensor.matmul(bank[:, h * HALF : (h + 1) * HALF], lhsT=ones[:], rhs=bias_row[:, h * HALF : (h + 1) * HALF], start=True, stop=True)

        def copy_bias():
            nc.scalar.copy(out=bias[:], in_=give_bank("bias")[:])

        def cols(gs):
            return slice(gs[0] * HALF, (gs[-1] + 1) * HALF)

        def widen(i, gs):
            for j in range(4 * gs[0], 4 * gs[-1] + 4):
                src = c_raw[i][:, j * P : (j + 1) * P].bitcast(FP8)
                dst = c_wide[i][:, j * P : (j + 1) * P]
                s = cs[:, i * TILES + j : i * TILES + j + 1]
                if i in WIDEN_ON_VECTOR:
                    nc.vector.tensor_scalar(out=dst, in0=src, scalar1=s, scalar2=None, op0=ALU.mult)
                else:
                    nc.scalar.activation(out=dst, in_=src, func=ACT.Copy, scale=s)

        def turn_c(i, gs):
            bank = take_bank(("tc", i, gs))
            for n in range(WARM if len(uses) == 1 else int(i in WARM_TILES)):
                nc.tensor.matmul(bank[:], lhsT=ones[:], rhs=zeros[:], start=True, stop=True)
            pairs = c_wide[i][:].bitcast(F32)
            for g in gs:
                for u in range(2):
                    slot = 2 * g + u
                    nc.tensor.transpose(bank[:, slot * P : (slot + 1) * P], pairs[:, 256 * g + u : 256 * (g + 1) : 2], ident[:])

        def turn_y(i, gs):
            bank = take_bank(("ty", i, gs))
            pairs = y_rows[i][:].bitcast(F32)
            for g in gs:
                for u in range(2):
                    slot = 2 * g + u
                    nc.tensor.transpose(bank[:, slot * P : (slot + 1) * P], pairs[:, slot * P : (slot + 1) * P], ident[:])

        def copy_turned(key, dst, gs):
            bank = give_bank(key)
            lo, hi = gs[0], gs[-1] + 1
            nc.scalar.copy(
                out=dst[:].bitcast(F32).rearrange("p (g r u) -> p g r u", g=2, u=2)[:, lo:hi],
                in_=bank[:].rearrange("p (g u r) -> p g r u", g=2, u=2)[:, lo:hi],
            )

        def quantize(src, dst, plane, gs):
            w = slice(gs[0] * P, (gs[-1] + 1) * P)
            nc.vector.quantize_mx(out=dst[:, w].bitcast(FP8X4), scales=plane[:, w], in_=src[:, cols(gs)])

        def product(k, i, h):
            bank = take_bank((k, i, h))
            act_codes, act_plane = (y_codes[i], y_plane[i]) if k == "f" else (c_codes[i], c_plane[i])
            for g in range(2):
                nc.tensor.matmul_mx(
                    out=bank[:],
                    lhsT=act_codes[:, g * P : (g + 1) * P].bitcast(FP8X4),
                    lhsT_scale=act_plane[:, g * P : (g + 1) * P],
                    rhs=codes[k, h][:, g, :].bitcast(FP8X4),
                    rhs_scale=planes[k][4 * g :, h * HALF : (h + 1) * HALF],
                    start=(g == 0),
                    stop=(g == 1),
                )

        def row_sum(i):
            if i in SUM_ON_VECTOR:
                nc.vector.tensor_scalar(out=junk_v[:], in0=x_sb[i], scalar1=1.0 / D, scalar2=None, op0=ALU.mult, op1=ALU.add, accum_out=mean[i][:, 0:1])

        def stats(i):
            if i in BN_ON_VECTOR:
                for h in range(2):
                    nc.vector.bn_stats(out=parts[i][:, 6 * h : 6 * h + 6], in_=x_sb[i][:, h * HALF : (h + 1) * HALF])
                nc.vector.bn_aggr(out=mean[i][:], in_=parts[i][:])
            else:
                if i not in SUM_ON_VECTOR:
                    nc.scalar.activation(out=junk_s[:, 0, :], in_=x_sb[i], func=ACT.Copy, scale=1.0 / D, accum_out=mean[i][:, 0:1])
                nc.scalar.activation(out=junk_s[:, 1, :], in_=x_sb[i], func=ACT.Square, scale=-1.0, bias=mean[i][:, 0:1], accum_out=ssq[i][:])

        def std(i):
            if i in BN_ON_VECTOR:
                nc.scalar.activation(out=veps[i][:], in_=mean[i][:, 1:2], func=ACT.Sqrt, scale=1.0, bias=EPS)
            else:
                nc.scalar.activation(out=veps[i][:], in_=ssq[i][:], func=ACT.Sqrt, scale=1.0 / D, bias=EPS)

        def inverse_std(i):
            nc.vector.reciprocal(out=rstd[i][:], in_=veps[i][:])

        def copy_scale(i, h):
            nc.scalar.copy(out=mod[i][:, cols((h,))], in_=give_bank(("sc", i, h))[:])

        def add_bias(i, h):
            n = cols((h,))
            if 2 * i + h in BIAS_ON_POOL:
                nc.gpsimd.tensor_tensor(out=mod[i][:, n], in0=mod[i][:, n], in1=bias[:, n], op=ALU.add)
            else:
                nc.vector.tensor_tensor(out=mod[i][:, n], in0=give_bank(("sc", i, h))[:], in1=bias[:, n], op=ALU.add)

        def modulate(i, h):
            n = cols((h,))
            nc.vector.scalar_tensor_tensor(out=mod[i][:, n], in0=x_sb[i][:, n], scalar=mean[i][:, 0:1], in1=mod[i][:, n], op0=ALU.subtract, op1=ALU.mult)

        def make_y(i, h):
            bank = give_bank(("sh", i, h))
            for u in range(2):
                slot = 2 * h + u
                nc.vector.scalar_tensor_tensor(
                    out=y_rows[i][:, 256 * slot : 256 * (slot + 1)].rearrange("p (m e) -> p m e", e=2),
                    in0=mod[i][:, cols((h,))].rearrange("p (m u e) -> p u m e", u=2, e=2)[:, u],
                    scalar=rstd[i][:],
                    in1=bank[:].rearrange("p (m u e) -> p u m e", u=2, e=2)[:, u],
                    op0=ALU.mult,
                    op1=ALU.add,
                )

        def copy_gate(i, h):
            nc.scalar.copy(out=gate[i][:, cols((h,))], in_=give_bank(("g", i, h))[:])

        def apply_gate(i, h):
            n = cols((h,))
            nc.vector.tensor_tensor(out=gate[i][:, n], in0=give_bank(("f", i, h))[:], in1=gate[i][:, n], op=ALU.mult)

        def finish(i, gs):
            n = cols(gs)
            engine = nc.vector if len(gs) == 1 and 2 * i + gs[0] in ADD_ON_VECTOR else nc.gpsimd
            if i in Q34:
                engine, n = ((nc.gpsimd, slice(0, 768)), (nc.vector, slice(768, D)))[gs[0]]
            engine.tensor_tensor(out=mod[i][:, n], in0=gate[i][:, n], in1=x_sb[i][:, n], op=ALU.add)
            nc.sync.dma_start(out=out[i * P : (i + 1) * P, n], in_=mod[i][:, n])

        stages = {
            "Wd": lambda i, gs: widen(i, gs),
            "Tc": lambda i, gs: turn_c(i, gs),
            "Cc": lambda i, gs: copy_turned(("tc", i, gs), c_turn[i], gs),
            "Qc": lambda i, gs: quantize(c_turn[i], c_codes[i], c_plane[i], gs),
            "Msc": lambda i, gs: product("sc", i, gs[0]),
            "Msh": lambda i, gs: product("sh", i, gs[0]),
            "Mg": lambda i, gs: product("g", i, gs[0]),
            "Mf": lambda i, gs: product("f", i, gs[0]),
            "aS": lambda i, gs: copy_scale(i, gs[0]),
            "a": lambda i, gs: add_bias(i, gs[0]),
            "Su": lambda i, gs: row_sum(i),
            "St": lambda i, gs: stats(i),
            "rs": lambda i, gs: std(i),
            "rc": lambda i, gs: inverse_std(i),
            "b": lambda i, gs: modulate(i, gs[0]),
            "c": lambda i, gs: make_y(i, gs[0]),
            "Ty": lambda i, gs: turn_y(i, gs),
            "Cy": lambda i, gs: copy_turned(("ty", i, gs), y_turn[i], gs),
            "Qy": lambda i, gs: quantize(y_turn[i], y_codes[i], y_plane[i], gs),
            "G": lambda i, gs: copy_gate(i, gs[0]),
            "gf": lambda i, gs: apply_gate(i, gs[0]),
            "add": lambda i, gs: finish(i, gs),
            "Mb": lambda i, gs: spread_bias(),
            "Cb": lambda i, gs: copy_bias(),
        }
        for name, gs, i in ORDER:
            stages[name](i, gs)
